import numpy as np
import ml_dtypes


def mxq(x, axis, fmt="e4m3"):
    dtype, down = {"e4m3": (ml_dtypes.float8_e4m3fn, 7), "e5m2": (ml_dtypes.float8_e5m2, 14)}[fmt]
    v = np.moveaxis(np.asarray(x, np.float32).astype(ml_dtypes.bfloat16).astype(np.float64), axis, -1)
    blocks = v.reshape(v.shape[:-1] + (-1, 32))
    amax = np.abs(blocks).max(-1, keepdims=True)
    byte = np.maximum(np.where(amax > 0, np.frexp(amax)[1] - 1 + 127, 0) - down, 1)
    scale = np.exp2(byte - 127.0)
    codes = (blocks / scale).astype(np.float32).astype(dtype).astype(np.float64)
    return np.moveaxis((codes * scale).reshape(v.shape), -1, axis)


WIDE = False


def mx_kscale(k):
    if not WIDE:
        return np.ones(k)
    levels = np.array([24, -24, 12, -12, 0])
    if k % 512:
        return np.exp2(np.random.permutation(np.resize(levels, k // 32))).repeat(32)
    a = np.empty((k // 512, 16))
    for p in range(k // 512):
        a[p, :8] = np.random.permutation(np.resize(levels, 8))
        for g in range(8):
            far = levels[np.abs(levels - a[p, g]) >= 10]
            a[p, g + 8] = far[np.random.randint(len(far))]
    return np.exp2(a.ravel()).repeat(32)


def f64(x):
    return np.asarray(x).astype(np.float64)


def striped(idx):
    return np.tile(idx.reshape(-1, 16).T, (8, 1)).astype(np.uint16)


def unstriped(offs):
    return offs[:16].T.reshape(-1).astype(np.int64)


E2M1 = np.array([0.0, 0.5, 1.0, 1.5, 2.0, 3.0, 4.0, 6.0, -0.0, -0.5, -1.0, -1.5, -2.0, -3.0, -4.0, -6.0])


def pack_weight(w, fmt):
    k, n = w.shape
    w = f64(np.asarray(w, np.float32).astype(ml_dtypes.bfloat16)).reshape(k // 32, 32, n)
    amax = np.abs(w).max(1)
    if fmt == "e4m3":
        byte = np.frexp(amax)[1] - 1 + 127 - 7
    else:
        mant, ex = np.frexp(amax / 6.0)
        byte = np.where(mant > 0.5, ex, ex - 1) + 127
    byte = np.clip(np.where(amax > 0, byte, 1), 1, 254)
    scaled = (w * np.exp2(127.0 - byte)[:, None, :]).reshape(k, n).astype(np.float32)
    by_word = np.ascontiguousarray(scaled.reshape(k // 512, 128, 4, n).transpose(0, 1, 3, 2))
    if fmt == "e4m3":
        words = by_word.astype(ml_dtypes.float8_e4m3fn).view(np.uint8)
    else:
        c = by_word.astype(ml_dtypes.float4_e2m1fn).view(np.uint8) & 0xF
        words = (c[..., 0::2] | (c[..., 1::2] << 4)).reshape(k // 512, 128, 2 * n)
    return np.ascontiguousarray(words), np.ascontiguousarray(byte.astype(np.uint8).reshape(k // 512, 16, n))


def unpack_weight(words, scales, fmt):
    g, _, n = scales.shape
    words = np.ascontiguousarray(words).reshape(g, 128, n, -1)
    if fmt == "e4m3":
        vals = words.view(ml_dtypes.float8_e4m3fn).astype(np.float64)
    else:
        nib = np.empty((g, 128, n, 4), np.uint8)
        nib[..., 0::2] = words & 0xF
        nib[..., 1::2] = words >> 4
        vals = E2M1[nib]
    vals = vals * np.repeat(np.exp2(scales.astype(np.float64) - 127.0), 8, axis=1)[..., None]
    return vals.transpose(0, 1, 3, 2).reshape(g * 512, n)


def pack_table4(v):
    words, scales = pack_weight(v, "e2m1")
    g, t = words.shape[0] // 2, v.shape[1]
    return np.ascontiguousarray(words.reshape(g, 2, 128, t, 2).transpose(0, 2, 3, 1, 4).reshape(g, 128, t, 4)), scales


def unpack_table4(words, scales):
    g, _, t, _ = words.shape
    return unpack_weight(words.reshape(g, 128, t, 2, 2).transpose(0, 3, 1, 2, 4).reshape(2 * g, 128, 2 * t), scales, "e2m1")


def silu(f):
    return f / (1.0 + np.exp(-np.maximum(f, -700.0)))


K, R, N, T, J = 1024, 1024, 512, 2048, 1024


def setup_inputs():
    n = np.random.standard_normal
    s = mx_kscale(K)[:, None]
    u = mx_kscale(R)[:, None]
    p_tab = pack_table4(n((K, T)) * s)
    p_wu = pack_weight(n((K, R)) / np.sqrt(K) / s, "e2m1")
    p_wd = pack_weight(n((R, N)) / np.sqrt(R) / u, "e4m3")
    return {
        "tab_words": p_tab[0],
        "tab_scales": p_tab[1],
        "wu_words": p_wu[0],
        "wu_scales": p_wu[1],
        "sm": (np.random.uniform(0.5, 2.0, R) * u[:, 0]).astype(np.float32),
        "wd_words": p_wd[0],
        "wd_scales": p_wd[1],
        "wgo": np.tile(np.random.uniform(0.5, 2.0, J), (128, 1)).astype(np.float32),
        "offs": striped(np.random.permutation(T)[:J]),
    }


def reference(tab_words, tab_scales, wu_words, wu_scales, sm, wd_words, wd_scales, wgo, offs):
    idx = unstriped(offs)
    tab_ = unpack_table4(tab_words, tab_scales)[:, idx]
    wu_ = unpack_weight(wu_words, wu_scales, "e2m1")
    a = wu_.T @ tab_
    h = f64(sm)[:, None] * silu(a)
    h_ = mxq(h, 0, "e4m3")
    wd_ = unpack_weight(wd_words, wd_scales, "e4m3")
    y = wd_.T @ h_
    out = np.zeros((N, T))
    out[:, idx] = f64(wgo)[0] * (y)
    return out

@@ -1,0 +1,248 @@
+from contextlib import ExitStack
+
+import concourse.mybir as mybir
+
+K, R, N, T, J = 1024, 1024, 512, 2048, 1024
+FLOPS = 2 * K * R * J + 2 * R * N * J
+
+F32 = mybir.dt.float32
+BF16 = mybir.dt.bfloat16
+I32 = mybir.dt.int32
+U32 = mybir.dt.uint32
+U16 = mybir.dt.uint16
+U8 = mybir.dt.uint8
+FP4X4 = mybir.dt.float4_e2m1fn_x4
+FP8X4 = mybir.dt.float8_e4m3fn_x4
+SILU = mybir.ActivationFunctionType.Silu
+COPY = mybir.ActivationFunctionType.Copy
+MULT = mybir.AluOpType.mult
+
+P = 128
+PACK = 4
+PASSES = 2
+CH = 256
+HALF = 128
+LANES = 16
+ROW0 = 96
+
+
+def tile_list_modp_silu_none_kernel(
+    tc, tab_words, tab_scales, wu_words, wu_scales, sm, wd_words, wd_scales, wgo, offs, out
+):
+    nc = tc.nc
+    with ExitStack() as ctx:
+        keep = ctx.enter_context(tc.tile_pool(name="keep", bufs=1))
+        work = ctx.enter_context(tc.tile_pool(name="work", bufs=2))
+        psum = ctx.enter_context(tc.psum_pool(name="psum", bufs=1))
+
+        def kept(shape, dtype, name, tag=None):
+            return keep.tile(shape, dtype, name=name, tag=tag or name, align_bytes=64)
+
+        offsets = keep.tile([P, J // LANES], U16, name="offsets")
+        nc.sync.dma_start(offsets[:], offs)
+        wu_rows = kept([P, R], U8, "wu_rows", "page1")
+        nc.sync.dma_start(wu_rows[ROW0:, :].bitcast(I32), wu_scales.rearrange("a q r -> q a r").bitcast(I32))
+        tab_rows = kept([P, T], U8, "tab_rows")
+        nc.sync.dma_start(tab_rows[ROW0:, :].bitcast(I32), tab_scales.rearrange("a q t -> q a t").bitcast(I32))
+        wu_raw = kept([P, PASSES, 2 * R], U8, "wu_raw", "wd")
+        nc.sync.dma_start(wu_raw[:].bitcast(I32), wu_words.rearrange("a p c -> p a c").bitcast(I32))
+        table = kept([P, T], I32, "table")
+        nc.sync.dma_start(table[:], tab_words[0].rearrange("p t i -> p (t i)").bitcast(I32))
+        smooth = kept([P, PASSES, PACK], F32, "smooth")
+        nc.sync.dma_start(smooth[:], sm.rearrange("(b p t) -> p b t", b=PASSES, t=PACK))
+
+        nc.vector.memset(wu_rows[:ROW0, :].bitcast(I32), 0)
+        nc.vector.memset(tab_rows[:ROW0, :].bitcast(I32), 0)
+        wu_planes = kept([P, PASSES, R], U8, "wu_planes")
+        nc.vector.memset(wu_planes[:].bitcast(I32), 0)
+        tab_planes = kept([P, PASSES, J], U8, "tab_planes")
+        nc.vector.memset(tab_planes[:].bitcast(I32), 0)
+        pages = [kept([P, T], F32, "page0")]
+        nc.vector.memset(pages[0][:], 0.0)
+
+        def spread_rows(planes, rows):
+            for q in range(4):
+                nc.scalar.dma_start(
+                    planes[32 * q : 32 * q + 4, :, :].bitcast(I32),
+                    rows[ROW0 + 8 * q : ROW0 + 8 * q + 8, :].bitcast(I32),
+                )
+
+        wu_rows_sorted = kept([P, R], U8, "wu_rows_sorted", "wd_planes")
+        nc.vector.tensor_copy(
+            wu_rows_sorted[:].rearrange("p (b t m) -> p b t m", b=PASSES, t=PACK),
+            wu_rows[:].rearrange("p (b m t) -> p b t m", b=PASSES, t=PACK),
+        )
+        spread_rows(wu_planes, wu_rows_sorted)
+        pages.append(kept([P, T], F32, "page1"))
+        nc.gpsimd.memset(pages[1][:], 0.0)
+        wd_planes = kept([P, N], U8, "wd_planes")
+        nc.gpsimd.memset(wd_planes[:].bitcast(I32), 0)
+
+        picked_rows = kept([P, J], U8, "picked_rows", "wgo")
+        nc.vector.tensor_copy(picked_rows[:], tab_rows[:].indirect(offsets[:]))
+        spread_rows(tab_planes, picked_rows)
+
+        wu_codes = []
+        for a in range(PASSES):
+            codes = kept([P, 2 * R], U8, "wu_codes%d" % a)
+            nc.vector.tensor_copy(
+                codes[:].bitcast(U16).rearrange("p (b t m) -> p b t m", b=PASSES, t=PACK),
+                wu_raw[:, a, :].bitcast(U16).rearrange("p (b m t) -> p b t m", b=PASSES, t=PACK),
+            )
+            wu_codes.append(codes)
+
+        wd_codes = kept([P, PASSES, N], I32, "wd_codes", "wd")
+        nc.sync.dma_start(wd_codes[:], wd_words.rearrange("a p n i -> p a (n i)").bitcast(I32))
+        for q in range(4):
+            nc.sync.dma_start(
+                wd_planes[32 * q : 32 * q + 8, :].bitcast(I32), wd_scales[:, 4 * q : 4 * q + 4, :].bitcast(I32)
+            )
+        gate = kept([P, J], F32, "gate", "wgo")
+        nc.sync.dma_start(gate[:], wgo)
+
+        def listed(j0, count):
+            return offsets[:, j0 // LANES : (j0 + count) // LANES]
+
+        def pick_words(j0, count):
+            pairs = kept([P, count], U32, "pairs%d" % j0)
+            nc.vector.tensor_copy(pairs[:], table[:].bitcast(U32).indirect(listed(j0, count)))
+            parted = kept([P, PASSES, 2 * count], U8, "parted%d" % j0)
+            nc.vector.tensor_copy(
+                parted[:].bitcast(U16), pairs[:].bitcast(U16).rearrange("p (j d) -> p d j", d=PASSES)
+            )
+            return parted
+
+        def up_product(bank_slice, tile, parted, first, j0, count):
+            cols = slice(tile * P, (tile + 1) * P)
+            for a in range(PASSES):
+                nc.tensor.matmul_mx(
+                    out=bank_slice,
+                    lhsT=wu_codes[a][:, 2 * cols.start : 2 * cols.stop].bitcast(FP4X4),
+                    lhsT_scale=wu_planes[:, a, cols],
+                    rhs=parted[:, a, 2 * (j0 - first) : 2 * (j0 - first + count)].bitcast(FP4X4),
+                    rhs_scale=tab_planes[:, a, j0 : j0 + count],
+                    start=(a == 0),
+                    stop=(a == PASSES - 1),
+                )
+
+        def fused_hidden(parted, first, c, b, hidden):
+            for half in range(CH // HALF):
+                bank = psum.tile([P, PACK, HALF], F32, name="up_bank", tag="up_bank", bufs=6)
+                for t in range(PACK):
+                    up_product(bank[:, t, :], b * PACK + t, parted, first, c * CH + half * HALF, HALF)
+                act = work.tile([P, HALF, PACK], F32, name="act", tag="act", bufs=6)
+                nc.scalar.activation(act[:], bank[:].rearrange("p t j -> p j t"), SILU)
+                nc.vector.tensor_tensor(
+                    hidden[:, b, half * HALF : (half + 1) * HALF, :],
+                    act[:],
+                    smooth[:, b, :].unsqueeze(1).broadcast_to([P, HALF, PACK]),
+                    MULT,
+                )
+
+        def activate(parted, first, c, pair):
+            bank = psum.tile([P, 2, CH], F32, name="up_bank", tag="up_bank", bufs=6)
+            for u in range(2):
+                up_product(bank[:, u, :], 2 * pair + u, parted, first, c * CH, CH)
+            act = work.tile([P, 2, CH], F32, name="act", tag="act", bufs=6)
+            nc.scalar.activation(act[:], bank[:], SILU)
+            return act
+
+        def smooth_rows(acts, b):
+            rows = work.tile([P, PACK, CH], BF16, name="rows", tag="rows", bufs=3)
+            for t in range(PACK):
+                nc.scalar.activation(rows[:, t, :], acts[2 * b + t // 2][:, t % 2, :], COPY, scale=smooth[:, b, t : t + 1])
+            return rows
+
+        def weave(engine_copy, hidden, rows, b):
+            engine_copy(
+                hidden[:, b, :, :].rearrange("p (c i) t -> p c t i", i=4),
+                rows[:].rearrange("p t (c i) -> p c t i", i=4),
+            )
+
+        def quantise(hidden, c, tag):
+            codes = kept([P, PASSES * CH], U32, "h_codes%d" % c, tag)
+            planes = kept([P, PASSES * CH], U8, "h_planes%d" % c)
+            nc.vector.quantize_mx(
+                out=codes[:].bitcast(FP8X4), scales=planes[:], in_=hidden[:].rearrange("p b j t -> p (b j t)")
+            )
+            return codes, planes
+
+        def down_product(quantised, pair):
+            codes, planes = quantised
+            bank = psum.tile([P, 2, CH], F32, name="down_bank", tag="down_bank", bufs=2)
+            for u in range(2):
+                cols = slice((2 * pair + u) * P, (2 * pair + u + 1) * P)
+                for a in range(PASSES):
+                    nc.tensor.matmul_mx(
+                        out=bank[:, u, :],
+                        lhsT=wd_codes[:, a, cols].bitcast(FP8X4),
+                        lhsT_scale=wd_planes[4 * a :, cols],
+                        rhs=codes[:, a * CH : (a + 1) * CH].bitcast(FP8X4),
+                        rhs_scale=planes[:, a * CH : (a + 1) * CH],
+                        start=(a == 0),
+                        stop=(a == PASSES - 1),
+                    )
+            return bank
+
+        results = [kept([P, 2, J], F32, "results%d" % pair) for pair in range(2)]
+
+        def leave(bank, c, pair):
+            nc.scalar.copy(results[pair][:, :, c * CH : (c + 1) * CH], bank[:])
+
+        def place(n, j0, count):
+            nc.vector.tensor_tensor(
+                pages[n][:].indirect(listed(j0, count)),
+                results[n // 2][:, n % 2, j0 : j0 + count],
+                gate[:, j0 : j0 + count],
+                MULT,
+            )
+
+        def store(n):
+            nc.sync.dma_start(out[n * P : (n + 1) * P, :], pages[n][:])
+
+        parted0 = pick_words(0, CH)
+        parted1 = pick_words(CH, CH)
+        hidden = kept([P, PASSES, CH, PACK], BF16, "hidden0", "page2")
+        for b in range(PASSES):
+            fused_hidden(parted0, 0, 0, b, hidden)
+        quantised = quantise(hidden, 0, "page3")
+        pages.append(kept([P, T], F32, "page2"))
+        nc.gpsimd.memset(pages[2][:], 0.0)
+        early = down_product(quantised, 0)
+        late = down_product(quantised, 1)
+        pages.append(kept([P, T], F32, "page3"))
+        nc.gpsimd.memset(pages[3][:], 0.0)
+        leave(early, 0, 0)
+        hidden = work.tile([P, PASSES, CH, PACK], BF16, name="hidden", tag="hidden", align_bytes=64)
+        fused_hidden(parted1, CH, 1, 0, hidden)
+        parted23 = pick_words(2 * CH, 2 * CH)
+        place(0, 0, CH)
+        place(1, 0, CH)
+
+        acts = [None, None] + [activate(parted1, CH, 1, pair) for pair in (2, 3)]
+        for c in range(1, 4):
+            passes = range(1 if c == 1 else 0, PASSES)
+            rows = {b: smooth_rows(acts, b) for b in passes}
+            for b in passes:
+                weave(nc.scalar.copy, hidden, rows[b], b)
+            quantised = quantise(hidden, c, None)
+            leave(late, c - 1, 1)
+            early = down_product(quantised, 0)
+            late = down_product(quantised, 1)
+            if c < 3:
+                place(2, (c - 1) * CH, CH)
+                place(3, (c - 1) * CH, CH)
+                acts = [activate(parted23, 2 * CH, c + 1, pair) for pair in range(3)]
+                leave(early, c, 0)
+                acts.append(activate(parted23, 2 * CH, c + 1, 3))
+                place(0, c * CH, CH)
+                place(1, c * CH, CH)
+                hidden = work.tile([P, PASSES, CH, PACK], BF16, name="hidden", tag="hidden", align_bytes=64)
+        place(2, 2 * CH, CH)
+        leave(early, 3, 0)
+        leave(late, 3, 1)
+        for n in range(3):
+            place(n, 3 * CH, CH)
+            store(n)
+        place(3, 2 * CH, 2 * CH)
+        store(3)

@@ -147,8 +147,8 @@ def tile_list_modp_silu_none_kernel(
             nc.scalar.activation(act[:], bank[:], SILU)
             return act
 
-        def smooth_rows(acts, b):
-            rows = work.tile([P, PACK, CH], BF16, name="rows", tag="rows", bufs=3)
+        def smooth_rows(acts, c, b):
+            rows = kept([P, PACK, CH], BF16, "rows%d%d" % (c, b))
             for t in range(PACK):
                 nc.scalar.activation(rows[:, t, :], acts[2 * b + t // 2][:, t % 2, :], COPY, scale=smooth[:, b, t : t + 1])
             return rows
@@ -184,18 +184,16 @@ def tile_list_modp_silu_none_kernel(
                     )
             return bank
 
-        results = [kept([P, 2, J], F32, "results%d" % pair) for pair in range(2)]
+        early_results = kept([P, 2, J], F32, "early_results")
 
-        def leave(bank, c, pair):
-            nc.scalar.copy(results[pair][:, :, c * CH : (c + 1) * CH], bank[:])
+        def place(n, values, j0, count):
+            nc.vector.tensor_tensor(pages[n][:].indirect(listed(j0, count)), values, gate[:, j0 : j0 + count], MULT)
 
-        def place(n, j0, count):
-            nc.vector.tensor_tensor(
-                pages[n][:].indirect(listed(j0, count)),
-                results[n // 2][:, n % 2, j0 : j0 + count],
-                gate[:, j0 : j0 + count],
-                MULT,
-            )
+        def leave_early(bank, c):
+            nc.scalar.copy(early_results[:, :, c * CH : (c + 1) * CH], bank[:])
+
+        def place_early(n, c):
+            place(n, early_results[:, n, c * CH : (c + 1) * CH], c * CH, CH)
 
         def store(n):
             nc.sync.dma_start(out[n * P : (n + 1) * P, :], pages[n][:])
@@ -212,37 +210,39 @@ def tile_list_modp_silu_none_kernel(
         late = down_product(quantised, 1)
         pages.append(kept([P, T], F32, "page3"))
         nc.gpsimd.memset(pages[3][:], 0.0)
-        leave(early, 0, 0)
+        leave_early(early, 0)
         hidden = work.tile([P, PASSES, CH, PACK], BF16, name="hidden", tag="hidden", align_bytes=64)
         fused_hidden(parted1, CH, 1, 0, hidden)
         parted23 = pick_words(2 * CH, 2 * CH)
-        place(0, 0, CH)
-        place(1, 0, CH)
+        place_early(0, 0)
+        place_early(1, 0)
 
         acts = [None, None] + [activate(parted1, CH, 1, pair) for pair in (2, 3)]
         for c in range(1, 4):
             passes = range(1 if c == 1 else 0, PASSES)
-            rows = {b: smooth_rows(acts, b) for b in passes}
+            rows = {b: smooth_rows(acts, c, b) for b in passes}
             for b in passes:
                 weave(nc.scalar.copy, hidden, rows[b], b)
             quantised = quantise(hidden, c, None)
-            leave(late, c - 1, 1)
+            late_results = kept([P, 2, CH if c < 3 else 2 * CH], F32, "late_results%d" % c, "rows%d1" % c)
+            nc.scalar.copy(late_results[:, :, :CH], late[:])
             early = down_product(quantised, 0)
             late = down_product(quantised, 1)
+            place(2, late_results[:, 0, :CH], (c - 1) * CH, CH)
             if c < 3:
-                place(2, (c - 1) * CH, CH)
-                place(3, (c - 1) * CH, CH)
+                place(3, late_results[:, 1, :CH], (c - 1) * CH, CH)
                 acts = [activate(parted23, 2 * CH, c + 1, pair) for pair in range(3)]
-                leave(early, c, 0)
+                leave_early(early, c)
                 acts.append(activate(parted23, 2 * CH, c + 1, 3))
-                place(0, c * CH, CH)
-                place(1, c * CH, CH)
+                place_early(0, c)
+                place_early(1, c)
                 hidden = work.tile([P, PASSES, CH, PACK], BF16, name="hidden", tag="hidden", align_bytes=64)
-        place(2, 2 * CH, CH)
-        leave(early, 3, 0)
-        leave(late, 3, 1)
-        for n in range(3):
-            place(n, 3 * CH, CH)
+        leave_early(early, 3)
+        nc.scalar.copy(late_results[:, :, CH:], late[:])
+        for n in range(2):
+            place_early(n, 3)
             store(n)
-        place(3, 2 * CH, 2 * CH)
+        place(2, late_results[:, 0, CH:], 3 * CH, CH)
+        store(2)
+        place(3, late_results[:, 1, :], 2 * CH, 2 * CH)
         store(3)

@@ -38,49 +38,61 @@ def tile_list_modp_silu_none_kernel(
         def kept(shape, dtype, name, tag=None):
             return keep.tile(shape, dtype, name=name, tag=tag or name, align_bytes=64)
 
+        def listed(j0, count):
+            return offsets[:, j0 // LANES : (j0 + count) // LANES]
+
         offsets = keep.tile([P, J // LANES], U16, name="offsets")
         nc.sync.dma_start(offsets[:], offs)
-        wu_rows = kept([P, R], U8, "wu_rows", "page1")
-        nc.sync.dma_start(wu_rows[ROW0:, :].bitcast(I32), wu_scales.rearrange("a q r -> q a r").bitcast(I32))
         tab_rows = kept([P, T], U8, "tab_rows")
         nc.sync.dma_start(tab_rows[ROW0:, :].bitcast(I32), tab_scales.rearrange("a q t -> q a t").bitcast(I32))
-        wu_raw = kept([P, PASSES, 2 * R], U8, "wu_raw", "wd")
+        wu_rows = kept([P, R], U8, "wu_rows")
+        nc.sync.dma_start(wu_rows[ROW0:, :].bitcast(I32), wu_scales.rearrange("a q r -> q a r").bitcast(I32))
+        wu_raw = kept([P, PASSES, 2 * R], U8, "wu_raw")
         nc.sync.dma_start(wu_raw[:].bitcast(I32), wu_words.rearrange("a p c -> p a c").bitcast(I32))
         table = kept([P, T], I32, "table")
         nc.sync.dma_start(table[:], tab_words[0].rearrange("p t i -> p (t i)").bitcast(I32))
         smooth = kept([P, PASSES, PACK], F32, "smooth")
         nc.sync.dma_start(smooth[:], sm.rearrange("(b p t) -> p b t", b=PASSES, t=PACK))
 
-        nc.vector.memset(wu_rows[:ROW0, :].bitcast(I32), 0)
         nc.vector.memset(tab_rows[:ROW0, :].bitcast(I32), 0)
+        nc.vector.memset(wu_rows[:ROW0, :].bitcast(I32), 0)
+        first_planes = kept([P, PASSES, CH], U8, "first_planes")
+        nc.vector.memset(first_planes[:].bitcast(I32), 0)
         wu_planes = kept([P, PASSES, R], U8, "wu_planes")
         nc.vector.memset(wu_planes[:].bitcast(I32), 0)
-        tab_planes = kept([P, PASSES, J], U8, "tab_planes")
-        nc.vector.memset(tab_planes[:].bitcast(I32), 0)
+        other_planes = kept([P, PASSES, J - CH], U8, "other_planes")
+        nc.vector.memset(other_planes[:].bitcast(I32), 0)
         pages = [kept([P, T], F32, "page0")]
         nc.vector.memset(pages[0][:], 0.0)
 
-        def spread_rows(planes, rows):
+        def spread_rows(queue, planes, rows):
             for q in range(4):
-                nc.scalar.dma_start(
+                queue.dma_start(
                     planes[32 * q : 32 * q + 4, :, :].bitcast(I32),
                     rows[ROW0 + 8 * q : ROW0 + 8 * q + 8, :].bitcast(I32),
                 )
 
-        wu_rows_sorted = kept([P, R], U8, "wu_rows_sorted", "wd_planes")
+        def pick_scales(queue, planes, j0, count, tag):
+            picked = kept([P, count], U8, "picked%d" % j0, tag)
+            nc.vector.tensor_copy(picked[:], tab_rows[:].indirect(listed(j0, count)))
+            spread_rows(queue, planes, picked)
+
+        def pick_words(j0, count, tag):
+            pairs = kept([P, count], U32, "pairs%d" % j0, tag)
+            nc.vector.tensor_copy(pairs[:], table[:].bitcast(U32).indirect(listed(j0, count)))
+            parted = kept([P, PASSES, 2 * count], U8, "parted%d" % j0)
+            nc.vector.tensor_copy(
+                parted[:].bitcast(U16), pairs[:].bitcast(U16).rearrange("p (j d) -> p d j", d=PASSES)
+            )
+            return parted
+
+        pick_scales(nc.scalar, first_planes, 0, CH, "wd_planes")
+        wu_rows_sorted = kept([P, R], U8, "wu_rows_sorted", "wd_codes")
         nc.vector.tensor_copy(
             wu_rows_sorted[:].rearrange("p (b t m) -> p b t m", b=PASSES, t=PACK),
             wu_rows[:].rearrange("p (b m t) -> p b t m", b=PASSES, t=PACK),
         )
-        spread_rows(wu_planes, wu_rows_sorted)
-        pages.append(kept([P, T], F32, "page1"))
-        nc.gpsimd.memset(pages[1][:], 0.0)
-        wd_planes = kept([P, N], U8, "wd_planes")
-        nc.gpsimd.memset(wd_planes[:].bitcast(I32), 0)
-
-        picked_rows = kept([P, J], U8, "picked_rows", "wgo")
-        nc.vector.tensor_copy(picked_rows[:], tab_rows[:].indirect(offsets[:]))
-        spread_rows(tab_planes, picked_rows)
+        spread_rows(nc.scalar, wu_planes, wu_rows_sorted)
 
         wu_codes = []
         for a in range(PASSES):
@@ -91,26 +103,24 @@ def tile_list_modp_silu_none_kernel(
             )
             wu_codes.append(codes)
 
-        wd_codes = kept([P, PASSES, N], I32, "wd_codes", "wd")
-        nc.sync.dma_start(wd_codes[:], wd_words.rearrange("a p n i -> p a (n i)").bitcast(I32))
+        parted0 = pick_words(0, CH, "gate")
+        pick_scales(nc.sync, other_planes, CH, J - CH, "gate")
+
+        wd_planes = kept([P, N], U8, "wd_planes")
+        nc.gpsimd.memset(wd_planes[:].bitcast(I32), 0)
         for q in range(4):
             nc.sync.dma_start(
                 wd_planes[32 * q : 32 * q + 8, :].bitcast(I32), wd_scales[:, 4 * q : 4 * q + 4, :].bitcast(I32)
             )
-        gate = kept([P, J], F32, "gate", "wgo")
+        wd_codes = kept([P, PASSES, N], I32, "wd_codes")
+        nc.sync.dma_start(wd_codes[:], wd_words.rearrange("a p n i -> p a (n i)").bitcast(I32))
+        gate = kept([P, J], F32, "gate")
         nc.sync.dma_start(gate[:], wgo)
 
-        def listed(j0, count):
-            return offsets[:, j0 // LANES : (j0 + count) // LANES]
-
-        def pick_words(j0, count):
-            pairs = kept([P, count], U32, "pairs%d" % j0)
-            nc.vector.tensor_copy(pairs[:], table[:].bitcast(U32).indirect(listed(j0, count)))
-            parted = kept([P, PASSES, 2 * count], U8, "parted%d" % j0)
-            nc.vector.tensor_copy(
-                parted[:].bitcast(U16), pairs[:].bitcast(U16).rearrange("p (j d) -> p d j", d=PASSES)
-            )
-            return parted
+        def table_scales(a, j0, count):
+            if j0 < CH:
+                return first_planes[:, a, j0 : j0 + count]
+            return other_planes[:, a, j0 - CH : j0 - CH + count]
 
         def up_product(bank_slice, tile, parted, first, j0, count):
             cols = slice(tile * P, (tile + 1) * P)
@@ -120,7 +130,7 @@ def tile_list_modp_silu_none_kernel(
                     lhsT=wu_codes[a][:, 2 * cols.start : 2 * cols.stop].bitcast(FP4X4),
                     lhsT_scale=wu_planes[:, a, cols],
                     rhs=parted[:, a, 2 * (j0 - first) : 2 * (j0 - first + count)].bitcast(FP4X4),
-                    rhs_scale=tab_planes[:, a, j0 : j0 + count],
+                    rhs_scale=table_scales(a, j0, count),
                     start=(a == 0),
                     stop=(a == PASSES - 1),
                 )
@@ -148,16 +158,13 @@ def tile_list_modp_silu_none_kernel(
             return act
 
         def smooth_rows(acts, c, b):
-            rows = kept([P, PACK, CH], BF16, "rows%d%d" % (c, b))
+            rows = kept([P, PACK, CH], BF16, "rows%d" % c)
             for t in range(PACK):
-                nc.scalar.activation(rows[:, t, :], acts[2 * b + t // 2][:, t % 2, :], COPY, scale=smooth[:, b, t : t + 1])
+                nc.scalar.activation(rows[:, t, :], acts[t // 2][:, t % 2, :], COPY, scale=smooth[:, b, t : t + 1])
             return rows
 
         def weave(engine_copy, hidden, rows, b):
-            engine_copy(
-                hidden[:, b, :, :].rearrange("p (c i) t -> p c t i", i=4),
-                rows[:].rearrange("p t (c i) -> p c t i", i=4),
-            )
+            engine_copy(hidden[:, b, :, :], rows[:].rearrange("p t j -> p j t"))
 
         def quantise(hidden, c, tag):
             codes = kept([P, PASSES * CH], U32, "h_codes%d" % c, tag)
@@ -198,45 +205,44 @@ def tile_list_modp_silu_none_kernel(
         def store(n):
             nc.sync.dma_start(out[n * P : (n + 1) * P, :], pages[n][:])
 
-        parted0 = pick_words(0, CH)
-        parted1 = pick_words(CH, CH)
-        hidden = kept([P, PASSES, CH, PACK], BF16, "hidden0", "page2")
+        parted1 = pick_words(CH, CH, None)
+        hidden = kept([P, PASSES, CH, PACK], BF16, "hidden0", "page1")
         for b in range(PASSES):
             fused_hidden(parted0, 0, 0, b, hidden)
-        quantised = quantise(hidden, 0, "page3")
-        pages.append(kept([P, T], F32, "page2"))
-        nc.gpsimd.memset(pages[2][:], 0.0)
+        quantised = quantise(hidden, 0, "page2")
+        pages.append(kept([P, T], F32, "page1"))
+        nc.gpsimd.memset(pages[1][:], 0.0)
         early = down_product(quantised, 0)
         late = down_product(quantised, 1)
-        pages.append(kept([P, T], F32, "page3"))
-        nc.gpsimd.memset(pages[3][:], 0.0)
+        pages.append(kept([P, T], F32, "page2"))
+        nc.gpsimd.memset(pages[2][:], 0.0)
         leave_early(early, 0)
-        hidden = work.tile([P, PASSES, CH, PACK], BF16, name="hidden", tag="hidden", align_bytes=64)
+        hidden = kept([P, PASSES, CH, PACK], BF16, "hidden1", "page3")
         fused_hidden(parted1, CH, 1, 0, hidden)
-        parted23 = pick_words(2 * CH, 2 * CH)
+        parted23 = pick_words(2 * CH, 2 * CH, None)
         place_early(0, 0)
         place_early(1, 0)
 
-        acts = [None, None] + [activate(parted1, CH, 1, pair) for pair in (2, 3)]
+        acts = [activate(parted1, CH, 1, pair) for pair in (2, 3)]
         for c in range(1, 4):
-            passes = range(1 if c == 1 else 0, PASSES)
-            rows = {b: smooth_rows(acts, c, b) for b in passes}
-            for b in passes:
-                weave(nc.scalar.copy, hidden, rows[b], b)
+            weave(nc.scalar.copy, hidden, smooth_rows(acts, c, 1), 1)
             quantised = quantise(hidden, c, None)
-            late_results = kept([P, 2, CH if c < 3 else 2 * CH], F32, "late_results%d" % c, "rows%d1" % c)
+            if c == 1:
+                pages.append(kept([P, T], F32, "page3"))
+                nc.gpsimd.memset(pages[3][:], 0.0)
+            late_results = kept([P, 2, CH if c < 3 else 2 * CH], F32, "late_results%d" % c, "rows%d" % c)
             nc.scalar.copy(late_results[:, :, :CH], late[:])
             early = down_product(quantised, 0)
             late = down_product(quantised, 1)
             place(2, late_results[:, 0, :CH], (c - 1) * CH, CH)
             if c < 3:
                 place(3, late_results[:, 1, :CH], (c - 1) * CH, CH)
-                acts = [activate(parted23, 2 * CH, c + 1, pair) for pair in range(3)]
+                hidden = kept([P, PASSES, CH, PACK], BF16, "hidden%d" % (c + 1))
+                fused_hidden(parted23, 2 * CH, c + 1, 0, hidden)
                 leave_early(early, c)
-                acts.append(activate(parted23, 2 * CH, c + 1, 3))
+                acts = [activate(parted23, 2 * CH, c + 1, pair) for pair in (2, 3)]
                 place_early(0, c)
                 place_early(1, c)
-                hidden = work.tile([P, PASSES, CH, PACK], BF16, name="hidden", tag="hidden", align_bytes=64)
         leave_early(early, 3)
         nc.scalar.copy(late_results[:, :, CH:], late[:])
         for n in range(2):

@@ -24,6 +24,7 @@ CH = 256
 HALF = 128
 LANES = 16
 ROW0 = 96
+FUSED = (1,)
 
 
 def tile_list_modp_silu_none_kernel(
@@ -43,31 +44,32 @@ def tile_list_modp_silu_none_kernel(
 
         offsets = keep.tile([P, J // LANES], U16, name="offsets")
         nc.sync.dma_start(offsets[:], offs)
-        tab_rows = kept([P, T], U8, "tab_rows")
-        nc.sync.dma_start(tab_rows[ROW0:, :].bitcast(I32), tab_scales.rearrange("a q t -> q a t").bitcast(I32))
         wu_rows = kept([P, R], U8, "wu_rows")
         nc.sync.dma_start(wu_rows[ROW0:, :].bitcast(I32), wu_scales.rearrange("a q r -> q a r").bitcast(I32))
-        wu_raw = kept([P, PASSES, 2 * R], U8, "wu_raw")
-        nc.sync.dma_start(wu_raw[:].bitcast(I32), wu_words.rearrange("a p c -> p a c").bitcast(I32))
+        tab_rows = kept([P, T], U8, "tab_rows")
+        nc.sync.dma_start(tab_rows[ROW0:, :].bitcast(I32), tab_scales.rearrange("a q t -> q a t").bitcast(I32))
+        wu_raw = [kept([P, 2 * R], U8, "wu_raw0", "gate"), kept([P, 2 * R], U8, "wu_raw1", "page1")]
+        for a in range(PASSES):
+            nc.sync.dma_start(wu_raw[a][:].bitcast(I32), wu_words[a].bitcast(I32))
         table = kept([P, T], I32, "table")
         nc.sync.dma_start(table[:], tab_words[0].rearrange("p t i -> p (t i)").bitcast(I32))
         smooth = kept([P, PASSES, PACK], F32, "smooth")
         nc.sync.dma_start(smooth[:], sm.rearrange("(b p t) -> p b t", b=PASSES, t=PACK))
 
-        nc.vector.memset(tab_rows[:ROW0, :].bitcast(I32), 0)
         nc.vector.memset(wu_rows[:ROW0, :].bitcast(I32), 0)
-        first_planes = kept([P, PASSES, CH], U8, "first_planes")
-        nc.vector.memset(first_planes[:].bitcast(I32), 0)
+        nc.vector.memset(tab_rows[:ROW0, :].bitcast(I32), 0)
         wu_planes = kept([P, PASSES, R], U8, "wu_planes")
         nc.vector.memset(wu_planes[:].bitcast(I32), 0)
+        first_planes = kept([P, PASSES, CH], U8, "first_planes")
+        nc.vector.memset(first_planes[:].bitcast(I32), 0)
         other_planes = kept([P, PASSES, J - CH], U8, "other_planes")
         nc.vector.memset(other_planes[:].bitcast(I32), 0)
         pages = [kept([P, T], F32, "page0")]
-        nc.vector.memset(pages[0][:], 0.0)
+        nc.gpsimd.memset(pages[0][:], 0.0)
 
-        def spread_rows(queue, planes, rows):
+        def spread_rows(queues, planes, rows):
             for q in range(4):
-                queue.dma_start(
+                queues[q].dma_start(
                     planes[32 * q : 32 * q + 4, :, :].bitcast(I32),
                     rows[ROW0 + 8 * q : ROW0 + 8 * q + 8, :].bitcast(I32),
                 )
@@ -75,7 +77,7 @@ def tile_list_modp_silu_none_kernel(
         def pick_scales(queue, planes, j0, count, tag):
             picked = kept([P, count], U8, "picked%d" % j0, tag)
             nc.vector.tensor_copy(picked[:], tab_rows[:].indirect(listed(j0, count)))
-            spread_rows(queue, planes, picked)
+            spread_rows([queue] * 4, planes, picked)
 
         def pick_words(j0, count, tag):
             pairs = kept([P, count], U32, "pairs%d" % j0, tag)
@@ -86,25 +88,27 @@ def tile_list_modp_silu_none_kernel(
             )
             return parted
 
-        pick_scales(nc.scalar, first_planes, 0, CH, "wd_planes")
         wu_rows_sorted = kept([P, R], U8, "wu_rows_sorted", "wd_codes")
         nc.vector.tensor_copy(
             wu_rows_sorted[:].rearrange("p (b t m) -> p b t m", b=PASSES, t=PACK),
             wu_rows[:].rearrange("p (b m t) -> p b t m", b=PASSES, t=PACK),
         )
-        spread_rows(nc.scalar, wu_planes, wu_rows_sorted)
+        spread_rows([nc.scalar] * 4, wu_planes, wu_rows_sorted)
+        pick_scales(nc.scalar, first_planes, 0, CH, "wd_planes")
 
         wu_codes = []
         for a in range(PASSES):
             codes = kept([P, 2 * R], U8, "wu_codes%d" % a)
             nc.vector.tensor_copy(
                 codes[:].bitcast(U16).rearrange("p (b t m) -> p b t m", b=PASSES, t=PACK),
-                wu_raw[:, a, :].bitcast(U16).rearrange("p (b m t) -> p b t m", b=PASSES, t=PACK),
+                wu_raw[a][:].bitcast(U16).rearrange("p (b m t) -> p b t m", b=PASSES, t=PACK),
             )
             wu_codes.append(codes)
 
-        parted0 = pick_words(0, CH, "gate")
+        pages.append(kept([P, T], F32, "page1"))
+        nc.gpsimd.memset(pages[1][:], 0.0)
         pick_scales(nc.sync, other_planes, CH, J - CH, "gate")
+        parted0 = pick_words(0, CH, "pairs")
 
         wd_planes = kept([P, N], U8, "wd_planes")
         nc.gpsimd.memset(wd_planes[:].bitcast(I32), 0)
@@ -158,9 +162,9 @@ def tile_list_modp_silu_none_kernel(
             return act
 
         def smooth_rows(acts, c, b):
-            rows = kept([P, PACK, CH], BF16, "rows%d" % c)
+            rows = kept([P, PACK, CH], BF16, "rows%d%d" % (c, b))
             for t in range(PACK):
-                nc.scalar.activation(rows[:, t, :], acts[t // 2][:, t % 2, :], COPY, scale=smooth[:, b, t : t + 1])
+                nc.scalar.activation(rows[:, t, :], acts[2 * b + t // 2][:, t % 2, :], COPY, scale=smooth[:, b, t : t + 1])
             return rows
 
         def weave(engine_copy, hidden, rows, b):
@@ -174,21 +178,27 @@ def tile_list_modp_silu_none_kernel(
             )
             return codes, planes
 
-        def down_product(quantised, pair):
+        def down_bank():
+            return psum.tile([P, 2, CH], F32, name="down_bank", tag="down_bank", bufs=2)
+
+        def down_tile(bank, quantised, n):
             codes, planes = quantised
-            bank = psum.tile([P, 2, CH], F32, name="down_bank", tag="down_bank", bufs=2)
-            for u in range(2):
-                cols = slice((2 * pair + u) * P, (2 * pair + u + 1) * P)
-                for a in range(PASSES):
-                    nc.tensor.matmul_mx(
-                        out=bank[:, u, :],
-                        lhsT=wd_codes[:, a, cols].bitcast(FP8X4),
-                        lhsT_scale=wd_planes[4 * a :, cols],
-                        rhs=codes[:, a * CH : (a + 1) * CH].bitcast(FP8X4),
-                        rhs_scale=planes[:, a * CH : (a + 1) * CH],
-                        start=(a == 0),
-                        stop=(a == PASSES - 1),
-                    )
+            cols = slice(n * P, (n + 1) * P)
+            for a in range(PASSES):
+                nc.tensor.matmul_mx(
+                    out=bank[:, n % 2, :],
+                    lhsT=wd_codes[:, a, cols].bitcast(FP8X4),
+                    lhsT_scale=wd_planes[4 * a :, cols],
+                    rhs=codes[:, a * CH : (a + 1) * CH].bitcast(FP8X4),
+                    rhs_scale=planes[:, a * CH : (a + 1) * CH],
+                    start=(a == 0),
+                    stop=(a == PASSES - 1),
+                )
+
+        def down_product(quantised, pair):
+            bank = down_bank()
+            for n in (2 * pair, 2 * pair + 1):
+                down_tile(bank, quantised, n)
             return bank
 
         early_results = kept([P, 2, J], F32, "early_results")
@@ -206,31 +216,40 @@ def tile_list_modp_silu_none_kernel(
             nc.sync.dma_start(out[n * P : (n + 1) * P, :], pages[n][:])
 
         parted1 = pick_words(CH, CH, None)
-        hidden = kept([P, PASSES, CH, PACK], BF16, "hidden0", "page1")
+        hidden = kept([P, PASSES, CH, PACK], BF16, "hidden0", "page2")
+        codes = kept([P, PASSES * CH], U32, "h_codes0", "page3")
+        planes = kept([P, PASSES * CH], U8, "h_planes0")
         for b in range(PASSES):
             fused_hidden(parted0, 0, 0, b, hidden)
-        quantised = quantise(hidden, 0, "page2")
-        pages.append(kept([P, T], F32, "page1"))
-        nc.gpsimd.memset(pages[1][:], 0.0)
-        early = down_product(quantised, 0)
-        late = down_product(quantised, 1)
+            nc.vector.quantize_mx(
+                out=codes[:, b * CH : (b + 1) * CH].bitcast(FP8X4),
+                scales=planes[:, b * CH : (b + 1) * CH],
+                in_=hidden[:, b, :, :].rearrange("p j t -> p (j t)"),
+            )
+        quantised = (codes, planes)
         pages.append(kept([P, T], F32, "page2"))
         nc.gpsimd.memset(pages[2][:], 0.0)
-        leave_early(early, 0)
-        hidden = kept([P, PASSES, CH, PACK], BF16, "hidden1", "page3")
+        early = down_bank()
+        for n in range(2):
+            down_tile(early, quantised, n)
+            nc.scalar.copy(early_results[:, n, :CH], early[:, n, :])
+        late = down_product(quantised, 1)
+        pages.append(kept([P, T], F32, "page3"))
+        nc.gpsimd.memset(pages[3][:], 0.0)
+        hidden = kept([P, PASSES, CH, PACK], BF16, "hidden1")
         fused_hidden(parted1, CH, 1, 0, hidden)
-        parted23 = pick_words(2 * CH, 2 * CH, None)
+        parted23 = pick_words(2 * CH, 2 * CH, "pairs")
         place_early(0, 0)
         place_early(1, 0)
 
-        acts = [activate(parted1, CH, 1, pair) for pair in (2, 3)]
+        acts = {pair: activate(parted1, CH, 1, pair) for pair in (2, 3)}
         for c in range(1, 4):
-            weave(nc.scalar.copy, hidden, smooth_rows(acts, c, 1), 1)
+            passes = range(1 if c in FUSED else 0, PASSES)
+            rows = {b: smooth_rows(acts, c, b) for b in passes}
+            for b in passes:
+                weave(nc.scalar.copy, hidden, rows[b], b)
             quantised = quantise(hidden, c, None)
-            if c == 1:
-                pages.append(kept([P, T], F32, "page3"))
-                nc.gpsimd.memset(pages[3][:], 0.0)
-            late_results = kept([P, 2, CH if c < 3 else 2 * CH], F32, "late_results%d" % c, "rows%d" % c)
+            late_results = kept([P, 2, CH if c < 3 else 2 * CH], F32, "late_results%d" % c, "rows%d1" % c)
             nc.scalar.copy(late_results[:, :, :CH], late[:])
             early = down_product(quantised, 0)
             late = down_product(quantised, 1)
@@ -238,9 +257,15 @@ def tile_list_modp_silu_none_kernel(
             if c < 3:
                 place(3, late_results[:, 1, :CH], (c - 1) * CH, CH)
                 hidden = kept([P, PASSES, CH, PACK], BF16, "hidden%d" % (c + 1))
-                fused_hidden(parted23, 2 * CH, c + 1, 0, hidden)
+                acts = {}
+                if c + 1 in FUSED:
+                    fused_hidden(parted23, 2 * CH, c + 1, 0, hidden)
+                else:
+                    for pair in (0, 1):
+                        acts[pair] = activate(parted23, 2 * CH, c + 1, pair)
+                acts[2] = activate(parted23, 2 * CH, c + 1, 2)
                 leave_early(early, c)
-                acts = [activate(parted23, 2 * CH, c + 1, pair) for pair in (2, 3)]
+                acts[3] = activate(parted23, 2 * CH, c + 1, 3)
                 place_early(0, c)
                 place_early(1, c)
         leave_early(early, 3)

@@ -20,11 +20,14 @@ MULT = mybir.AluOpType.mult
 P = 128
 PACK = 4
 PASSES = 2
+QUADRANTS = 4
 CH = 256
 HALF = 128
+LAST = J // CH - 1
 LANES = 16
 ROW0 = 96
-FUSED = (1,)
+UP_BANKS = 6
+DOWN_BANKS = 2
 
 
 def tile_list_modp_silu_none_kernel(
@@ -33,11 +36,11 @@ def tile_list_modp_silu_none_kernel(
     nc = tc.nc
     with ExitStack() as ctx:
         keep = ctx.enter_context(tc.tile_pool(name="keep", bufs=1))
-        work = ctx.enter_context(tc.tile_pool(name="work", bufs=2))
+        work = ctx.enter_context(tc.tile_pool(name="work", bufs=UP_BANKS))
         psum = ctx.enter_context(tc.psum_pool(name="psum", bufs=1))
 
-        def kept(shape, dtype, name, tag=None):
-            return keep.tile(shape, dtype, name=name, tag=tag or name, align_bytes=64)
+        def kept(shape, dtype, name, slot=None):
+            return keep.tile(shape, dtype, name=name, tag=slot or name, align_bytes=64)
 
         def listed(j0, count):
             return offsets[:, j0 // LANES : (j0 + count) // LANES]
@@ -48,7 +51,7 @@ def tile_list_modp_silu_none_kernel(
         nc.sync.dma_start(wu_rows[ROW0:, :].bitcast(I32), wu_scales.rearrange("a q r -> q a r").bitcast(I32))
         tab_rows = kept([P, T], U8, "tab_rows")
         nc.sync.dma_start(tab_rows[ROW0:, :].bitcast(I32), tab_scales.rearrange("a q t -> q a t").bitcast(I32))
-        wu_raw = [kept([P, 2 * R], U8, "wu_raw0", "gate"), kept([P, 2 * R], U8, "wu_raw1", "page1")]
+        wu_raw = [kept([P, 2 * R], U8, "wu_raw0", "gate"), kept([P, 2 * R], U8, "wu_raw1")]
         for a in range(PASSES):
             nc.sync.dma_start(wu_raw[a][:].bitcast(I32), wu_words[a].bitcast(I32))
         table = kept([P, T], I32, "table")
@@ -64,23 +67,24 @@ def tile_list_modp_silu_none_kernel(
         nc.vector.memset(first_planes[:].bitcast(I32), 0)
         other_planes = kept([P, PASSES, J - CH], U8, "other_planes")
         nc.vector.memset(other_planes[:].bitcast(I32), 0)
-        pages = [kept([P, T], F32, "page0")]
-        nc.gpsimd.memset(pages[0][:], 0.0)
+        pages = [kept([P, T], F32, "page%d" % n) for n in range(2)]
+        for page in pages:
+            nc.vector.memset(page[:], 0.0)
 
-        def spread_rows(queues, planes, rows):
-            for q in range(4):
-                queues[q].dma_start(
-                    planes[32 * q : 32 * q + 4, :, :].bitcast(I32),
-                    rows[ROW0 + 8 * q : ROW0 + 8 * q + 8, :].bitcast(I32),
+        def spread_rows(queue, planes, rows):
+            for quad in range(QUADRANTS):
+                queue.dma_start(
+                    planes[32 * quad : 32 * quad + 4, :, :].bitcast(I32),
+                    rows[ROW0 + 8 * quad : ROW0 + 8 * quad + 8, :].bitcast(I32),
                 )
 
-        def pick_scales(queue, planes, j0, count, tag):
-            picked = kept([P, count], U8, "picked%d" % j0, tag)
+        def pick_scales(queue, planes, j0, count, slot):
+            picked = kept([P, count], U8, "picked%d" % j0, slot)
             nc.vector.tensor_copy(picked[:], tab_rows[:].indirect(listed(j0, count)))
-            spread_rows([queue] * 4, planes, picked)
+            spread_rows(queue, planes, picked)
 
-        def pick_words(j0, count, tag):
-            pairs = kept([P, count], U32, "pairs%d" % j0, tag)
+        def pick_words(j0, count, slot):
+            pairs = kept([P, count], U32, "pairs%d" % j0, slot)
             nc.vector.tensor_copy(pairs[:], table[:].bitcast(U32).indirect(listed(j0, count)))
             parted = kept([P, PASSES, 2 * count], U8, "parted%d" % j0)
             nc.vector.tensor_copy(
@@ -88,63 +92,60 @@ def tile_list_modp_silu_none_kernel(
             )
             return parted
 
+        def sort_columns(target, source):
+            nc.vector.tensor_copy(
+                target.rearrange("p (b t m) -> p b t m", b=PASSES, t=PACK),
+                source.rearrange("p (b m t) -> p b t m", b=PASSES, t=PACK),
+            )
+
         wu_rows_sorted = kept([P, R], U8, "wu_rows_sorted", "wd_codes")
-        nc.vector.tensor_copy(
-            wu_rows_sorted[:].rearrange("p (b t m) -> p b t m", b=PASSES, t=PACK),
-            wu_rows[:].rearrange("p (b m t) -> p b t m", b=PASSES, t=PACK),
-        )
-        spread_rows([nc.scalar] * 4, wu_planes, wu_rows_sorted)
+        sort_columns(wu_rows_sorted[:], wu_rows[:])
+        spread_rows(nc.sync, wu_planes, wu_rows_sorted)
         pick_scales(nc.scalar, first_planes, 0, CH, "wd_planes")
 
-        wu_codes = []
+        wu_codes = [kept([P, 2 * R], U8, "wu_codes%d" % a) for a in range(PASSES)]
         for a in range(PASSES):
-            codes = kept([P, 2 * R], U8, "wu_codes%d" % a)
-            nc.vector.tensor_copy(
-                codes[:].bitcast(U16).rearrange("p (b t m) -> p b t m", b=PASSES, t=PACK),
-                wu_raw[a][:].bitcast(U16).rearrange("p (b m t) -> p b t m", b=PASSES, t=PACK),
-            )
-            wu_codes.append(codes)
+            sort_columns(wu_codes[a][:].bitcast(U16), wu_raw[a][:].bitcast(U16))
 
-        pages.append(kept([P, T], F32, "page1"))
-        nc.gpsimd.memset(pages[1][:], 0.0)
         pick_scales(nc.sync, other_planes, CH, J - CH, "gate")
         parted0 = pick_words(0, CH, "pairs")
 
         wd_planes = kept([P, N], U8, "wd_planes")
         nc.gpsimd.memset(wd_planes[:].bitcast(I32), 0)
-        for q in range(4):
+        for quad in range(QUADRANTS):
             nc.sync.dma_start(
-                wd_planes[32 * q : 32 * q + 8, :].bitcast(I32), wd_scales[:, 4 * q : 4 * q + 4, :].bitcast(I32)
+                wd_planes[32 * quad : 32 * quad + 8, :].bitcast(I32),
+                wd_scales[:, 4 * quad : 4 * quad + 4, :].bitcast(I32),
             )
         wd_codes = kept([P, PASSES, N], I32, "wd_codes")
         nc.sync.dma_start(wd_codes[:], wd_words.rearrange("a p n i -> p a (n i)").bitcast(I32))
         gate = kept([P, J], F32, "gate")
         nc.sync.dma_start(gate[:], wgo)
 
-        def table_scales(a, j0, count):
+        def table_plane(a, j0, count):
             if j0 < CH:
                 return first_planes[:, a, j0 : j0 + count]
             return other_planes[:, a, j0 - CH : j0 - CH + count]
 
-        def up_product(bank_slice, tile, parted, first, j0, count):
-            cols = slice(tile * P, (tile + 1) * P)
+        def up_product(sums, wu_slice, parted, first, j0, count):
+            c0, c1 = wu_slice * P, (wu_slice + 1) * P
             for a in range(PASSES):
                 nc.tensor.matmul_mx(
-                    out=bank_slice,
-                    lhsT=wu_codes[a][:, 2 * cols.start : 2 * cols.stop].bitcast(FP4X4),
-                    lhsT_scale=wu_planes[:, a, cols],
+                    out=sums,
+                    lhsT=wu_codes[a][:, 2 * c0 : 2 * c1].bitcast(FP4X4),
+                    lhsT_scale=wu_planes[:, a, c0:c1],
                     rhs=parted[:, a, 2 * (j0 - first) : 2 * (j0 - first + count)].bitcast(FP4X4),
-                    rhs_scale=table_scales(a, j0, count),
+                    rhs_scale=table_plane(a, j0, count),
                     start=(a == 0),
                     stop=(a == PASSES - 1),
                 )
 
-        def fused_hidden(parted, first, c, b, hidden):
+        def hidden_on_vector(parted, c, b, hidden):
             for half in range(CH // HALF):
-                bank = psum.tile([P, PACK, HALF], F32, name="up_bank", tag="up_bank", bufs=6)
+                bank = psum.tile([P, PACK, HALF], F32, name="up_bank", tag="up_bank", bufs=UP_BANKS)
                 for t in range(PACK):
-                    up_product(bank[:, t, :], b * PACK + t, parted, first, c * CH + half * HALF, HALF)
-                act = work.tile([P, HALF, PACK], F32, name="act", tag="act", bufs=6)
+                    up_product(bank[:, t, :], b * PACK + t, parted, c * CH, c * CH + half * HALF, HALF)
+                act = work.tile([P, HALF, PACK], F32, name="act", tag="act")
                 nc.scalar.activation(act[:], bank[:].rearrange("p t j -> p j t"), SILU)
                 nc.vector.tensor_tensor(
                     hidden[:, b, half * HALF : (half + 1) * HALF, :],
@@ -153,127 +154,115 @@ def tile_list_modp_silu_none_kernel(
                     MULT,
                 )
 
-        def activate(parted, first, c, pair):
-            bank = psum.tile([P, 2, CH], F32, name="up_bank", tag="up_bank", bufs=6)
+        def activate(parted, first, c, duo):
+            bank = psum.tile([P, 2, CH], F32, name="up_bank", tag="up_bank", bufs=UP_BANKS)
             for u in range(2):
-                up_product(bank[:, u, :], 2 * pair + u, parted, first, c * CH, CH)
-            act = work.tile([P, 2, CH], F32, name="act", tag="act", bufs=6)
+                up_product(bank[:, u, :], 2 * duo + u, parted, first, c * CH, CH)
+            act = work.tile([P, 2, CH], F32, name="act", tag="act")
             nc.scalar.activation(act[:], bank[:], SILU)
             return act
 
-        def smooth_rows(acts, c, b):
-            rows = kept([P, PACK, CH], BF16, "rows%d%d" % (c, b))
+        def scale_slices(acts, c, b):
+            scaled = kept([P, PACK, CH], BF16, "scaled%d%d" % (c, b))
             for t in range(PACK):
-                nc.scalar.activation(rows[:, t, :], acts[2 * b + t // 2][:, t % 2, :], COPY, scale=smooth[:, b, t : t + 1])
-            return rows
+                nc.scalar.activation(
+                    scaled[:, t, :], acts[2 * b + t // 2][:, t % 2, :], COPY, scale=smooth[:, b, t : t + 1]
+                )
+            return scaled
 
-        def weave(engine_copy, hidden, rows, b):
-            engine_copy(hidden[:, b, :, :], rows[:].rearrange("p t j -> p j t"))
+        def h_tiles(c):
+            return kept([P, PASSES * CH], U32, "h_codes%d" % c), kept([P, PASSES * CH], U8, "h_planes%d" % c)
 
-        def quantise(hidden, c, tag):
-            codes = kept([P, PASSES * CH], U32, "h_codes%d" % c, tag)
-            planes = kept([P, PASSES * CH], U8, "h_planes%d" % c)
-            nc.vector.quantize_mx(
-                out=codes[:].bitcast(FP8X4), scales=planes[:], in_=hidden[:].rearrange("p b j t -> p (b j t)")
-            )
-            return codes, planes
+        def quantise(h_codes, h_planes, values):
+            nc.vector.quantize_mx(out=h_codes.bitcast(FP8X4), scales=h_planes, in_=values)
 
         def down_bank():
-            return psum.tile([P, 2, CH], F32, name="down_bank", tag="down_bank", bufs=2)
+            return psum.tile([P, 2, CH], F32, name="down_bank", tag="down_bank", bufs=DOWN_BANKS)
 
-        def down_tile(bank, quantised, n):
-            codes, planes = quantised
+        def down_product(bank, h_codes, h_planes, n):
             cols = slice(n * P, (n + 1) * P)
             for a in range(PASSES):
                 nc.tensor.matmul_mx(
                     out=bank[:, n % 2, :],
                     lhsT=wd_codes[:, a, cols].bitcast(FP8X4),
                     lhsT_scale=wd_planes[4 * a :, cols],
-                    rhs=codes[:, a * CH : (a + 1) * CH].bitcast(FP8X4),
-                    rhs_scale=planes[:, a * CH : (a + 1) * CH],
+                    rhs=h_codes[:, a * CH : (a + 1) * CH].bitcast(FP8X4),
+                    rhs_scale=h_planes[:, a * CH : (a + 1) * CH],
                     start=(a == 0),
                     stop=(a == PASSES - 1),
                 )
 
-        def down_product(quantised, pair):
+        def down_pair(h_codes, h_planes, n0):
             bank = down_bank()
-            for n in (2 * pair, 2 * pair + 1):
-                down_tile(bank, quantised, n)
+            for n in (n0, n0 + 1):
+                down_product(bank, h_codes, h_planes, n)
             return bank
 
-        early_results = kept([P, 2, J], F32, "early_results")
+        early_y = kept([P, 2, J], F32, "early_y")
 
         def place(n, values, j0, count):
             nc.vector.tensor_tensor(pages[n][:].indirect(listed(j0, count)), values, gate[:, j0 : j0 + count], MULT)
 
         def leave_early(bank, c):
-            nc.scalar.copy(early_results[:, :, c * CH : (c + 1) * CH], bank[:])
+            nc.scalar.copy(early_y[:, :, c * CH : (c + 1) * CH], bank[:])
 
         def place_early(n, c):
-            place(n, early_results[:, n, c * CH : (c + 1) * CH], c * CH, CH)
+            place(n, early_y[:, n, c * CH : (c + 1) * CH], c * CH, CH)
 
         def store(n):
             nc.sync.dma_start(out[n * P : (n + 1) * P, :], pages[n][:])
 
         parted1 = pick_words(CH, CH, None)
-        hidden = kept([P, PASSES, CH, PACK], BF16, "hidden0", "page2")
-        codes = kept([P, PASSES * CH], U32, "h_codes0", "page3")
-        planes = kept([P, PASSES * CH], U8, "h_planes0")
+        hidden = kept([P, PASSES, CH, PACK], BF16, "hidden0", "page3")
+        h_codes, h_planes = h_tiles(0)
         for b in range(PASSES):
-            fused_hidden(parted0, 0, 0, b, hidden)
-            nc.vector.quantize_mx(
-                out=codes[:, b * CH : (b + 1) * CH].bitcast(FP8X4),
-                scales=planes[:, b * CH : (b + 1) * CH],
-                in_=hidden[:, b, :, :].rearrange("p j t -> p (j t)"),
-            )
-        quantised = (codes, planes)
-        pages.append(kept([P, T], F32, "page2"))
-        nc.gpsimd.memset(pages[2][:], 0.0)
+            hidden_on_vector(parted0, 0, b, hidden)
+            cols = slice(b * CH, (b + 1) * CH)
+            quantise(h_codes[:, cols], h_planes[:, cols], hidden[:, b, :, :].rearrange("p j t -> p (j t)"))
         early = down_bank()
         for n in range(2):
-            down_tile(early, quantised, n)
-            nc.scalar.copy(early_results[:, n, :CH], early[:, n, :])
-        late = down_product(quantised, 1)
-        pages.append(kept([P, T], F32, "page3"))
-        nc.gpsimd.memset(pages[3][:], 0.0)
+            down_product(early, h_codes, h_planes, n)
+            nc.scalar.copy(early_y[:, n, :CH], early[:, n, :])
+        late = down_pair(h_codes, h_planes, 2)
         hidden = kept([P, PASSES, CH, PACK], BF16, "hidden1")
-        fused_hidden(parted1, CH, 1, 0, hidden)
+        hidden_on_vector(parted1, 1, 0, hidden)
         parted23 = pick_words(2 * CH, 2 * CH, "pairs")
+        pages.append(kept([P, T], F32, "page2", "pairs"))
+        pages.append(kept([P, T], F32, "page3"))
+        for page in pages[2:]:
+            nc.vector.memset(page[:], 0.0)
         place_early(0, 0)
         place_early(1, 0)
 
-        acts = {pair: activate(parted1, CH, 1, pair) for pair in (2, 3)}
-        for c in range(1, 4):
-            passes = range(1 if c in FUSED else 0, PASSES)
-            rows = {b: smooth_rows(acts, c, b) for b in passes}
-            for b in passes:
-                weave(nc.scalar.copy, hidden, rows[b], b)
-            quantised = quantise(hidden, c, None)
-            late_results = kept([P, 2, CH if c < 3 else 2 * CH], F32, "late_results%d" % c, "rows%d1" % c)
-            nc.scalar.copy(late_results[:, :, :CH], late[:])
-            early = down_product(quantised, 0)
-            late = down_product(quantised, 1)
-            place(2, late_results[:, 0, :CH], (c - 1) * CH, CH)
-            if c < 3:
-                place(3, late_results[:, 1, :CH], (c - 1) * CH, CH)
+        acts = {duo: activate(parted1, CH, 1, duo) for duo in (2, 3)}
+        for c in range(1, LAST + 1):
+            on_scalar = range(1 if c == 1 else 0, PASSES)
+            scaled = {b: scale_slices(acts, c, b) for b in on_scalar}
+            for b in on_scalar:
+                nc.scalar.copy(hidden[:, b, :, :], scaled[b][:].rearrange("p t j -> p j t"))
+            h_codes, h_planes = h_tiles(c)
+            quantise(h_codes[:], h_planes[:], hidden[:].rearrange("p b j t -> p (b j t)"))
+
+            late_y = kept([P, 2, CH if c < LAST else 2 * CH], F32, "late_y%d" % c, "scaled%d1" % c)
+            nc.scalar.copy(late_y[:, :, :CH], late[:])
+            early = down_pair(h_codes, h_planes, 0)
+            late = down_pair(h_codes, h_planes, 2)
+            place(2, late_y[:, 0, :CH], (c - 1) * CH, CH)
+            if c < LAST:
+                place(3, late_y[:, 1, :CH], (c - 1) * CH, CH)
                 hidden = kept([P, PASSES, CH, PACK], BF16, "hidden%d" % (c + 1))
-                acts = {}
-                if c + 1 in FUSED:
-                    fused_hidden(parted23, 2 * CH, c + 1, 0, hidden)
-                else:
-                    for pair in (0, 1):
-                        acts[pair] = activate(parted23, 2 * CH, c + 1, pair)
-                acts[2] = activate(parted23, 2 * CH, c + 1, 2)
+                acts = {duo: activate(parted23, 2 * CH, c + 1, duo) for duo in range(3)}
                 leave_early(early, c)
                 acts[3] = activate(parted23, 2 * CH, c + 1, 3)
                 place_early(0, c)
                 place_early(1, c)
-        leave_early(early, 3)
-        nc.scalar.copy(late_results[:, :, CH:], late[:])
+
+        leave_early(early, LAST)
+        nc.scalar.copy(late_y[:, :, CH:], late[:])
         for n in range(2):
-            place_early(n, 3)
+            place_early(n, LAST)
             store(n)
-        place(2, late_results[:, 0, CH:], 3 * CH, CH)
+        place(2, late_y[:, 0, CH:], LAST * CH, CH)
         store(2)
-        place(3, late_results[:, 1, :], 2 * CH, 2 * CH)
+        place(3, late_y[:, 1, :], (LAST - 1) * CH, 2 * CH)
         store(3)

from contextlib import ExitStack

import concourse.mybir as mybir

K, R, N, T, J = 1024, 1024, 512, 2048, 1024
FLOPS = 2 * K * R * J + 2 * R * N * J

F32 = mybir.dt.float32
BF16 = mybir.dt.bfloat16
I32 = mybir.dt.int32
U32 = mybir.dt.uint32
U16 = mybir.dt.uint16
U8 = mybir.dt.uint8
FP4X4 = mybir.dt.float4_e2m1fn_x4
FP8X4 = mybir.dt.float8_e4m3fn_x4
SILU = mybir.ActivationFunctionType.Silu
COPY = mybir.ActivationFunctionType.Copy
MULT = mybir.AluOpType.mult

P = 128
PACK = 4
PASSES = 2
QUADRANTS = 4
CH = 256
HALF = 128
LAST = J // CH - 1
LANES = 16
ROW0 = 96
UP_BANKS = 6
DOWN_BANKS = 2


def tile_list_modp_silu_none_kernel(
    tc, tab_words, tab_scales, wu_words, wu_scales, sm, wd_words, wd_scales, wgo, offs, out
):
    nc = tc.nc
    with ExitStack() as ctx:
        keep = ctx.enter_context(tc.tile_pool(name="keep", bufs=1))
        work = ctx.enter_context(tc.tile_pool(name="work", bufs=UP_BANKS))
        psum = ctx.enter_context(tc.psum_pool(name="psum", bufs=1))

        def kept(shape, dtype, name, slot=None):
            return keep.tile(shape, dtype, name=name, tag=slot or name, align_bytes=64)

        def listed(j0, count):
            return offsets[:, j0 // LANES : (j0 + count) // LANES]

        offsets = keep.tile([P, J // LANES], U16, name="offsets")
        nc.sync.dma_start(offsets[:], offs)
        wu_rows = kept([P, R], U8, "wu_rows")
        nc.sync.dma_start(wu_rows[ROW0:, :].bitcast(I32), wu_scales.rearrange("a q r -> q a r").bitcast(I32))
        tab_rows = kept([P, T], U8, "tab_rows")
        nc.sync.dma_start(tab_rows[ROW0:, :].bitcast(I32), tab_scales.rearrange("a q t -> q a t").bitcast(I32))
        wu_raw = [kept([P, 2 * R], U8, "wu_raw0", "gate"), kept([P, 2 * R], U8, "wu_raw1")]
        for a in range(PASSES):
            nc.sync.dma_start(wu_raw[a][:].bitcast(I32), wu_words[a].bitcast(I32))
        table = kept([P, T], I32, "table")
        nc.sync.dma_start(table[:], tab_words[0].rearrange("p t i -> p (t i)").bitcast(I32))
        smooth = kept([P, PASSES, PACK], F32, "smooth")
        nc.sync.dma_start(smooth[:], sm.rearrange("(b p t) -> p b t", b=PASSES, t=PACK))

        nc.vector.memset(wu_rows[:ROW0, :].bitcast(I32), 0)
        nc.vector.memset(tab_rows[:ROW0, :].bitcast(I32), 0)
        wu_planes = kept([P, PASSES, R], U8, "wu_planes")
        nc.vector.memset(wu_planes[:].bitcast(I32), 0)
        first_planes = kept([P, PASSES, CH], U8, "first_planes")
        nc.vector.memset(first_planes[:].bitcast(I32), 0)
        other_planes = kept([P, PASSES, J - CH], U8, "other_planes")
        nc.vector.memset(other_planes[:].bitcast(I32), 0)
        pages = [kept([P, T], F32, "page%d" % n) for n in range(2)]
        for page in pages:
            nc.vector.memset(page[:], 0.0)

        def spread_rows(queue, planes, rows):
            for quad in range(QUADRANTS):
                queue.dma_start(
                    planes[32 * quad : 32 * quad + 4, :, :].bitcast(I32),
                    rows[ROW0 + 8 * quad : ROW0 + 8 * quad + 8, :].bitcast(I32),
                )

        def pick_scales(queue, planes, j0, count, slot):
            picked = kept([P, count], U8, "picked%d" % j0, slot)
            nc.vector.tensor_copy(picked[:], tab_rows[:].indirect(listed(j0, count)))
            spread_rows(queue, planes, picked)

        def pick_words(j0, count, slot):
            pairs = kept([P, count], U32, "pairs%d" % j0, slot)
            nc.vector.tensor_copy(pairs[:], table[:].bitcast(U32).indirect(listed(j0, count)))
            parted = kept([P, PASSES, 2 * count], U8, "parted%d" % j0)
            nc.vector.tensor_copy(
                parted[:].bitcast(U16), pairs[:].bitcast(U16).rearrange("p (j d) -> p d j", d=PASSES)
            )
            return parted

        def sort_columns(target, source):
            nc.vector.tensor_copy(
                target.rearrange("p (b t m) -> p b t m", b=PASSES, t=PACK),
                source.rearrange("p (b m t) -> p b t m", b=PASSES, t=PACK),
            )

        wu_rows_sorted = kept([P, R], U8, "wu_rows_sorted", "wd_codes")
        sort_columns(wu_rows_sorted[:], wu_rows[:])
        spread_rows(nc.sync, wu_planes, wu_rows_sorted)
        pick_scales(nc.scalar, first_planes, 0, CH, "wd_planes")

        wu_codes = [kept([P, 2 * R], U8, "wu_codes%d" % a) for a in range(PASSES)]
        for a in range(PASSES):
            sort_columns(wu_codes[a][:].bitcast(U16), wu_raw[a][:].bitcast(U16))

        pick_scales(nc.sync, other_planes, CH, J - CH, "gate")
        parted0 = pick_words(0, CH, "pairs")

        wd_planes = kept([P, N], U8, "wd_planes")
        nc.gpsimd.memset(wd_planes[:].bitcast(I32), 0)
        for quad in range(QUADRANTS):
            nc.sync.dma_start(
                wd_planes[32 * quad : 32 * quad + 8, :].bitcast(I32),
                wd_scales[:, 4 * quad : 4 * quad + 4, :].bitcast(I32),
            )
        wd_codes = kept([P, PASSES, N], I32, "wd_codes")
        nc.sync.dma_start(wd_codes[:], wd_words.rearrange("a p n i -> p a (n i)").bitcast(I32))
        gate = kept([P, J], F32, "gate")
        nc.sync.dma_start(gate[:], wgo)

        def table_plane(a, j0, count):
            if j0 < CH:
                return first_planes[:, a, j0 : j0 + count]
            return other_planes[:, a, j0 - CH : j0 - CH + count]

        def up_product(sums, wu_slice, parted, first, j0, count):
            c0, c1 = wu_slice * P, (wu_slice + 1) * P
            for a in range(PASSES):
                nc.tensor.matmul_mx(
                    out=sums,
                    lhsT=wu_codes[a][:, 2 * c0 : 2 * c1].bitcast(FP4X4),
                    lhsT_scale=wu_planes[:, a, c0:c1],
                    rhs=parted[:, a, 2 * (j0 - first) : 2 * (j0 - first + count)].bitcast(FP4X4),
                    rhs_scale=table_plane(a, j0, count),
                    start=(a == 0),
                    stop=(a == PASSES - 1),
                )

        def hidden_on_vector(parted, c, b, hidden):
            for half in range(CH // HALF):
                bank = psum.tile([P, PACK, HALF], F32, name="up_bank", tag="up_bank", bufs=UP_BANKS)
                for t in range(PACK):
                    up_product(bank[:, t, :], b * PACK + t, parted, c * CH, c * CH + half * HALF, HALF)
                act = work.tile([P, HALF, PACK], F32, name="act", tag="act")
                nc.scalar.activation(act[:], bank[:].rearrange("p t j -> p j t"), SILU)
                nc.vector.tensor_tensor(
                    hidden[:, b, half * HALF : (half + 1) * HALF, :],
                    act[:],
                    smooth[:, b, :].unsqueeze(1).broadcast_to([P, HALF, PACK]),
                    MULT,
                )

        def activate(parted, first, c, duo):
            bank = psum.tile([P, 2, CH], F32, name="up_bank", tag="up_bank", bufs=UP_BANKS)
            for u in range(2):
                up_product(bank[:, u, :], 2 * duo + u, parted, first, c * CH, CH)
            act = work.tile([P, 2, CH], F32, name="act", tag="act")
            nc.scalar.activation(act[:], bank[:], SILU)
            return act

        def scale_slices(acts, c, b):
            scaled = kept([P, PACK, CH], BF16, "scaled%d%d" % (c, b))
            for t in range(PACK):
                nc.scalar.activation(
                    scaled[:, t, :], acts[2 * b + t // 2][:, t % 2, :], COPY, scale=smooth[:, b, t : t + 1]
                )
            return scaled

        def h_tiles(c):
            return kept([P, PASSES * CH], U32, "h_codes%d" % c), kept([P, PASSES * CH], U8, "h_planes%d" % c)

        def quantise(h_codes, h_planes, values):
            nc.vector.quantize_mx(out=h_codes.bitcast(FP8X4), scales=h_planes, in_=values)

        def down_bank():
            return psum.tile([P, 2, CH], F32, name="down_bank", tag="down_bank", bufs=DOWN_BANKS)

        def down_product(bank, h_codes, h_planes, n):
            cols = slice(n * P, (n + 1) * P)
            for a in range(PASSES):
                nc.tensor.matmul_mx(
                    out=bank[:, n % 2, :],
                    lhsT=wd_codes[:, a, cols].bitcast(FP8X4),
                    lhsT_scale=wd_planes[4 * a :, cols],
                    rhs=h_codes[:, a * CH : (a + 1) * CH].bitcast(FP8X4),
                    rhs_scale=h_planes[:, a * CH : (a + 1) * CH],
                    start=(a == 0),
                    stop=(a == PASSES - 1),
                )

        def down_pair(h_codes, h_planes, n0):
            bank = down_bank()
            for n in (n0, n0 + 1):
                down_product(bank, h_codes, h_planes, n)
            return bank

        early_y = kept([P, 2, J], F32, "early_y")

        def place(n, values, j0, count):
            nc.vector.tensor_tensor(pages[n][:].indirect(listed(j0, count)), values, gate[:, j0 : j0 + count], MULT)

        def leave_early(bank, c):
            nc.scalar.copy(early_y[:, :, c * CH : (c + 1) * CH], bank[:])

        def place_early(n, c):
            place(n, early_y[:, n, c * CH : (c + 1) * CH], c * CH, CH)

        def store(n):
            nc.sync.dma_start(out[n * P : (n + 1) * P, :], pages[n][:])

        parted1 = pick_words(CH, CH, None)
        hidden = kept([P, PASSES, CH, PACK], BF16, "hidden0", "page3")
        h_codes, h_planes = h_tiles(0)
        for b in range(PASSES):
            hidden_on_vector(parted0, 0, b, hidden)
            cols = slice(b * CH, (b + 1) * CH)
            quantise(h_codes[:, cols], h_planes[:, cols], hidden[:, b, :, :].rearrange("p j t -> p (j t)"))
        early = down_bank()
        for n in range(2):
            down_product(early, h_codes, h_planes, n)
            nc.scalar.copy(early_y[:, n, :CH], early[:, n, :])
        late = down_pair(h_codes, h_planes, 2)
        hidden = kept([P, PASSES, CH, PACK], BF16, "hidden1")
        hidden_on_vector(parted1, 1, 0, hidden)
        parted23 = pick_words(2 * CH, 2 * CH, "pairs")
        pages.append(kept([P, T], F32, "page2", "pairs"))
        pages.append(kept([P, T], F32, "page3"))
        for page in pages[2:]:
            nc.vector.memset(page[:], 0.0)
        place_early(0, 0)
        place_early(1, 0)

        acts = {duo: activate(parted1, CH, 1, duo) for duo in (2, 3)}
        for c in range(1, LAST + 1):
            on_scalar = range(1 if c == 1 else 0, PASSES)
            scaled = {b: scale_slices(acts, c, b) for b in on_scalar}
            for b in on_scalar:
                nc.scalar.copy(hidden[:, b, :, :], scaled[b][:].rearrange("p t j -> p j t"))
            h_codes, h_planes = h_tiles(c)
            quantise(h_codes[:], h_planes[:], hidden[:].rearrange("p b j t -> p (b j t)"))

            late_y = kept([P, 2, CH if c < LAST else 2 * CH], F32, "late_y%d" % c, "scaled%d1" % c)
            nc.scalar.copy(late_y[:, :, :CH], late[:])
            early = down_pair(h_codes, h_planes, 0)
            late = down_pair(h_codes, h_planes, 2)
            place(2, late_y[:, 0, :CH], (c - 1) * CH, CH)
            if c < LAST:
                place(3, late_y[:, 1, :CH], (c - 1) * CH, CH)
                hidden = kept([P, PASSES, CH, PACK], BF16, "hidden%d" % (c + 1))
                acts = {duo: activate(parted23, 2 * CH, c + 1, duo) for duo in range(3)}
                leave_early(early, c)
                acts[3] = activate(parted23, 2 * CH, c + 1, 3)
                place_early(0, c)
                place_early(1, c)

        leave_early(early, LAST)
        nc.scalar.copy(late_y[:, :, CH:], late[:])
        for n in range(2):
            place_early(n, LAST)
            store(n)
        place(2, late_y[:, 0, CH:], LAST * CH, CH)
        store(2)
        place(3, late_y[:, 1, :], (LAST - 1) * CH, 2 * CH)
        store(3)
